import numpy as np
import ml_dtypes


def mxq(x, axis, fmt="e4m3"):
    dtype, down = {"e4m3": (ml_dtypes.float8_e4m3fn, 7), "e5m2": (ml_dtypes.float8_e5m2, 14)}[fmt]
    v = np.moveaxis(np.asarray(x, np.float32).astype(ml_dtypes.bfloat16).astype(np.float64), axis, -1)
    blocks = v.reshape(v.shape[:-1] + (-1, 32))
    amax = np.abs(blocks).max(-1, keepdims=True)
    byte = np.maximum(np.where(amax > 0, np.frexp(amax)[1] - 1 + 127, 0) - down, 1)
    scale = np.exp2(byte - 127.0)
    codes = (blocks / scale).astype(np.float32).astype(dtype).astype(np.float64)
    return np.moveaxis((codes * scale).reshape(v.shape), -1, axis)


WIDE = False


def mx_kscale(k):
    if not WIDE:
        return np.ones(k)
    levels = np.array([10, -10, 5, -5, 0])
    if k % 512:
        return np.exp2(np.random.permutation(np.resize(levels, k // 32))).repeat(32)
    a = np.empty((k // 512, 16))
    for p in range(k // 512):
        a[p, :8] = np.random.permutation(np.resize(levels, 8))
        for g in range(8):
            far = levels[np.abs(levels - a[p, g]) >= 10]
            a[p, g + 8] = far[np.random.randint(len(far))]
    return np.exp2(a.ravel()).repeat(32)


def f64(x):
    return np.asarray(x).astype(np.float64)


def striped(idx):
    return np.tile(idx.reshape(-1, 16).T, (8, 1)).astype(np.uint16)


def unstriped(offs):
    return offs[:16].T.reshape(-1).astype(np.int64)


def striped8(idx):
    return np.concatenate([x.reshape(-1, 16).T for x in idx]).astype(np.uint16)


def runs(offs, k):
    lists = np.stack([offs[16 * r : 16 * r + 16].T.reshape(-1) for r in range(8)]).astype(np.int64)
    return lists[np.arange(k) % 512 // 64]


def pack_weight(w):
    k, n = w.shape
    w = f64(np.asarray(w, np.float32).astype(ml_dtypes.bfloat16)).reshape(k // 32, 32, n)
    amax = np.abs(w).max(1)
    byte = np.clip(np.where(amax > 0, np.frexp(amax)[1] - 1 + 127 - 7, 1), 1, 254)
    scaled = (w * np.exp2(127.0 - byte)[:, None, :]).reshape(k, n).astype(np.float32)
    words = np.ascontiguousarray(scaled.reshape(k // 512, 128, 4, n).transpose(0, 1, 3, 2)).astype(ml_dtypes.float8_e4m3fn).view(np.uint8)
    return words, np.ascontiguousarray(byte.astype(np.uint8).reshape(k // 512, 16, n))


def unpack_weight(words, scales):
    g, p, n, _ = words.shape
    vals = np.ascontiguousarray(words).view(ml_dtypes.float8_e4m3fn).astype(np.float64) * np.repeat(np.exp2(scales.astype(np.float64) - 127.0), 8, axis=1)[..., None]
    return vals.transpose(0, 1, 3, 2).reshape(g * 512, n)

def planes(y):
    n, m = y.shape
    v = y.astype(np.float32).astype(ml_dtypes.bfloat16).astype(np.float64).reshape(n // 32, 32, m)
    top = np.abs(v).max(1)
    byte = np.clip(np.where(top > 0, np.frexp(top)[1] - 1 + 127 - 7, 1), 1, 254)
    codes = (v * np.exp2(127.0 - byte)[:, None, :]).reshape(n, m).astype(np.float32).astype(ml_dtypes.float8_e4m3fn).view(np.uint8)
    words = codes.reshape(n // 512, 128, 4, m).transpose(0, 1, 3, 2)
    return np.ascontiguousarray(words), np.ascontiguousarray(byte.astype(np.uint8).reshape(n // 512, 16, m))


K, T, S, H, C = 512, 2048, 512, 512, 512


def setup_inputs():
    n = np.random.standard_normal
    s = mx_kscale(K)[:, None]
    packed_xT = pack_weight(n((K, T)) * s)
    packed_w1 = pack_weight(n((K, H)) / np.sqrt(K) / s)
    return {
        "x_words": packed_xT[0],
        "x_scales": packed_xT[1],
        "w1_words": packed_w1[0],
        "w1_scales": packed_w1[1],
        "gs": (np.random.uniform(0.5, 1.5, (K, 1)) / s).astype(np.float32),
        "gs2": (np.random.uniform(0.5, 1.5, (K, 1)) / s).astype(np.float32),
        "offs": striped(np.random.permutation(T)[:S]),
        "n1": striped(np.random.permutation(S)),
        "n2": striped(np.random.permutation(S)),
        "n3": striped8(np.stack([np.random.permutation(S) for _ in range(8)])),
        "n4": striped8(np.stack([np.random.permutation(S) for _ in range(8)])),
        "n5": striped8(np.stack([np.random.permutation(S) for _ in range(8)])),
        "n6": striped8(np.stack([np.random.permutation(S) for _ in range(8)])),
        "ca": striped(np.random.permutation(T)[:C]),
        "cb": striped(np.random.permutation(T)[:C]),
        "n7": striped8(np.stack([np.random.permutation(S) for _ in range(8)])),
        "n8": striped8(np.stack([np.random.permutation(S) for _ in range(8)])),
    }


def reference(x_words, x_scales, w1_words, w1_scales, gs, gs2, offs, n1, n2, n3, n4, n5, n6, ca, cb, n7, n8):
    x_ca = unpack_weight(x_words, x_scales)[:, unstriped(ca)]
    xq = unpack_weight(x_words, x_scales)[:, unstriped(offs)]
    y = unpack_weight(w1_words, w1_scales).T @ xq
    sq = (y) ** 2
    z = f64(gs) * (y[:, unstriped(n2)] / (np.sqrt(sq + sq[:, unstriped(n1)] + 0.25)))
    a = 0.0625 * ((x_ca.T @ mxq(z, 0, "e4m3")))
    x_cb = unpack_weight(x_words, x_scales)[:, unstriped(cb)]
    z2 = f64(gs2) * (0.75 * ((y[np.arange(H)[:, None], runs(n3, H)]) * (y[np.arange(H)[:, None], runs(n4, H)]) - ((y[np.arange(H)[:, None], runs(n5, H)]) * (y[np.arange(H)[:, None], runs(n6, H)]))))
    b = 0.0625 * ((x_cb.T @ mxq(z2, 0, "e4m3")))
    out_0 = 0.75 * (a * (b[np.arange(C)[:, None], runs(n8, C)]) - ((a[np.arange(C)[:, None], runs(n7, C)]) * b))
    return (out_0,) + planes(out_0)

@@ -1,0 +1,245 @@
+from contextlib import ExitStack
+
+import concourse.mybir as mybir
+
+K, T, S, H, C = 512, 2048, 512, 512, 512
+FLOPS = 2 * K * S * (H + 2 * C)
+
+F32 = mybir.dt.float32
+BF16 = mybir.dt.bfloat16
+I32 = mybir.dt.int32
+U32 = mybir.dt.uint32
+U16 = mybir.dt.uint16
+U8 = mybir.dt.uint8
+FP8X4 = mybir.dt.float8_e4m3fn_x4
+ACT = mybir.ActivationFunctionType
+MULT = mybir.AluOpType.mult
+ADD = mybir.AluOpType.add
+SUB = mybir.AluOpType.subtract
+
+P = 128
+PACK = 4
+HALF = S // 2
+SPARE = 16
+LCOL = S // 16
+
+
+def tile_picked_twocdcrossbrmsdet_none_po_kernel(
+    tc, x_words, x_scales, w1_words, w1_scales, gs, gs2, offs, n1, n2, n3, n4, n5, n6, ca, cb, n7, n8,
+    out_0, out_1, out_2,
+):
+    nc = tc.nc
+    with ExitStack() as ctx:
+        keep = ctx.enter_context(tc.tile_pool(name="keep", bufs=1))
+        psum = ctx.enter_context(tc.psum_pool(name="psum", bufs=1))
+
+        def load_list(name, src):
+            tile = keep.tile([P, LCOL], U16, name="list_" + name)
+            nc.sync.dma_start(tile[:], src)
+            return tile
+
+        def load_scales(engine, tile, src):
+            for q in range(4):
+                rows = src[0, 4 * q : 4 * q + 4, :].bitcast(I32)
+                engine.dma_start(tile[32 * q : 32 * q + 32, :].bitcast(I32), rows.partition_broadcast(8))
+
+        def half_cols(h):
+            return slice(h * HALF, (h + 1) * HALF)
+
+        def half_list(lst, h):
+            return lst[:, h * (LCOL // 2) : (h + 1) * (LCOL // 2)]
+
+        def deal(dst, src, run):
+            nc.vector.tensor_copy(
+                out=dst.rearrange("p (g t c i) -> p g c t i", t=PACK, c=P // run, i=run),
+                in_=src.rearrange("p (g c i t) -> p g c t i", t=PACK, c=P // run, i=run),
+            )
+
+        def woven(ap):
+            return ap.rearrange("p (c i t) -> p c t i", i=4, t=PACK)
+
+        def planar(ap):
+            return ap.rearrange("p t (c i) -> p c t i", i=4)
+
+        xs = keep.tile([P, T], U8, name="xs", align_bytes=64)
+        xw = keep.tile([P, T], U32, name="xw", align_bytes=64)
+        ww = keep.tile([P, H], U32, name="ww", align_bytes=64)
+        ws = keep.tile([P, H], U8, name="ws", align_bytes=64)
+        load_scales(nc.sync, xs, x_scales)
+        l_offs = load_list("offs", offs)
+        nc.sync.dma_start(ww[:].bitcast(I32), w1_words[0].rearrange("p n t -> p (n t)").bitcast(I32))
+        nc.sync.dma_start(xw[:].bitcast(I32), x_words[0].rearrange("p n t -> p (n t)").bitcast(I32))
+        l_ca = load_list("ca", ca)
+        load_scales(nc.sync, ws, w1_scales)
+        l_cb = load_list("cb", cb)
+        g1 = keep.tile([P, PACK], F32, name="g1")
+        g2raw = keep.tile([P, PACK], F32, name="g2raw")
+        nc.sync.dma_start(g1[:], gs.rearrange("(p t) o -> p (t o)", t=PACK))
+        nc.sync.dma_start(g2raw[:], gs2.rearrange("(p t) o -> p (t o)", t=PACK))
+        l_n1 = load_list("n1", n1)
+        l_n3 = load_list("n3", n3)
+        l_n5 = load_list("n5", n5)
+        l_n2 = load_list("n2", n2)
+        l_n4 = load_list("n4", n4)
+        l_n6 = load_list("n6", n6)
+        l_n7 = load_list("n7", n7)
+        l_n8 = load_list("n8", n8)
+
+        sq = [keep.tile([P, S + SPARE], F32, name=f"sq{t}") for t in range(PACK)]
+        yg = [keep.tile([P, S + SPARE], F32, name=f"yg{t}") for t in range(PACK)]
+        for t in range(PACK):
+            nc.gpsimd.memset(sq[t][:, S:], 0.0)
+            nc.gpsimd.memset(yg[t][:, S:], 0.0)
+
+        qw = keep.tile([P, S], U32, name="qw", align_bytes=64)
+        qs = keep.tile([P, S], U8, name="qs", tag="bytes0", align_bytes=64)
+        cw = keep.tile([P, 2 * C], U32, name="cw", align_bytes=64)
+        csa = keep.tile([P, C], U8, name="csa", align_bytes=64)
+        wwd = keep.tile([P, H], U32, name="wwd", align_bytes=64)
+        wsd = keep.tile([P, H], U8, name="wsd", align_bytes=64)
+        cwd = keep.tile([P, 2 * C], U32, name="cwd", align_bytes=64)
+        csd = keep.tile([P, 2 * C], U8, name="csd", align_bytes=64)
+        nc.vector.tensor_copy(qs[:], xs[:].indirect(l_offs[:]))
+        deal(wwd[:], ww[:], 4)
+        nc.vector.tensor_copy(qw[:], xw[:].indirect(l_offs[:]))
+        deal(wsd[:], ws[:], 16)
+        nc.vector.tensor_copy(csa[:], xs[:].indirect(l_ca[:]))
+        g2 = keep.tile([P, PACK], F32, name="g2")
+        nc.gpsimd.tensor_scalar(g2[:], g2raw[:], 0.75, 0.0, MULT, ADD)
+        nc.vector.tensor_copy(cw[:, :C], xw[:].indirect(l_ca[:]))
+        nc.vector.tensor_copy(cw[:, C:], xw[:].indirect(l_cb[:]))
+
+        y = [keep.tile([P, S], F32, name=f"y{t}") for t in range(PACK)]
+        yc = [keep.tile([P, S], F32, name=f"yc{t}") for t in range(PACK)]
+        sq2 = [keep.tile([P, S], F32, name=f"sq2_{t}") for t in range(PACK)]
+        for t in range(PACK):
+            cols = slice(t * P, (t + 1) * P)
+            bank = psum.tile([P, S], F32, name=f"ybank{t}", tag=f"yb{t}")
+            nc.tensor.matmul_mx(
+                out=bank[:], lhsT=wwd[:, cols].bitcast(FP8X4), lhsT_scale=wsd[:, cols],
+                rhs=qw[:].bitcast(FP8X4), rhs_scale=qs[:], start=True, stop=True,
+            )
+            nc.scalar.activation(sq[t][:, :S], bank[:], ACT.Square)
+            nc.sync.dma_start(sq2[t][:], sq[t][:, :S])
+            nc.scalar.copy(y[t][:], bank[:])
+            nc.gpsimd.tensor_scalar(yc[t][:], y[t][:], g2[:, t : t + 1], 0.0, MULT, ADD)
+            nc.gpsimd.tensor_scalar(yg[t][:, :S], y[t][:], g1[:, t : t + 1], 0.0, MULT, ADD)
+
+        csb = keep.tile([P, C], U8, name="csb", tag="bytes0", align_bytes=64)
+        nc.vector.tensor_copy(csb[:], xs[:].indirect(l_cb[:]))
+        deal(cwd[:], cw[:], 4)
+        deal(csd[:, :C], csa[:], 16)
+        deal(csd[:, C:], csb[:], 16)
+
+        ssum = [keep.tile([P, S], F32, name=f"ssum{t}") for t in range(PACK)]
+        rs = [keep.tile([P, S], F32, name=f"rs{t}") for t in range(PACK)]
+        zf = keep.tile([P, PACK, S], F32, name="zf")
+        y3 = [keep.tile([P, PACK, HALF], F32, name=f"y3_{h}") for h in range(2)]
+        y5 = [keep.tile([P, PACK, HALF], F32, name=f"y5_{h}") for h in range(2)]
+        for t in range(PACK):
+            nc.vector.tensor_tensor(ssum[t][:], sq[t][:].indirect(l_n1[:]), sq2[t][:], ADD)
+            nc.scalar.activation(y3[0][:, t, :], yc[t][:].indirect(half_list(l_n3, 0)), ACT.Copy)
+            nc.scalar.activation(rs[t][:], ssum[t][:], ACT.Abs_reciprocal_sqrt, bias=0.25)
+        for t in range(PACK):
+            nc.vector.tensor_tensor(zf[:, t, :], yg[t][:].indirect(l_n2[:]), rs[t][:], MULT)
+            nc.scalar.activation(y5[0][:, t, :], yc[t][:].indirect(half_list(l_n5, 0)), ACT.Copy)
+        zb = keep.tile([P, S * PACK], BF16, name="zb", align_bytes=64)
+        zw = keep.tile([P, S], U32, name="zw", align_bytes=64)
+        zs = keep.tile([P, S], U8, name="zs", align_bytes=64)
+        nc.scalar.copy(woven(zb[:]), planar(zf[:]))
+        for t in range(PACK):
+            nc.scalar.activation(y3[1][:, t, :], yc[t][:].indirect(half_list(l_n3, 1)), ACT.Copy)
+
+        p4 = [keep.tile([P, PACK, HALF], F32, name=f"p4_{h}") for h in range(2)]
+        p6 = [keep.tile([P, PACK, HALF], F32, name=f"p6_{h}") for h in range(2)]
+        z2b = [keep.tile([P, HALF * PACK], BF16, name=f"z2b{h}", align_bytes=64) for h in range(2)]
+        z2w = [keep.tile([P, HALF], U32, name=f"z2w{h}", align_bytes=64) for h in range(2)]
+        z2s = [keep.tile([P, HALF], U8, name=f"z2s{h}", align_bytes=64) for h in range(2)]
+        bbank = {}
+
+        def z2_first(h):
+            for t in range(PACK):
+                nc.vector.tensor_tensor(p4[h][:, t, :], y[t][:].indirect(half_list(l_n4, h)), y3[h][:, t, :], MULT)
+
+        def z2_second(h):
+            for t in range(PACK):
+                nc.vector.tensor_tensor(p6[h][:, t, :], y[t][:].indirect(half_list(l_n6, h)), y5[h][:, t, :], MULT)
+            nc.vector.tensor_tensor(woven(z2b[h][:]), planar(p4[h][:]), planar(p6[h][:]), SUB)
+
+        def z2_matmul(h):
+            nc.vector.quantize_mx(out=z2w[h][:].bitcast(FP8X4), scales=z2s[h][:], in_=z2b[h][:])
+            for u in range(2):
+                bank = psum.tile([P, 2, HALF], F32, name=f"bbank{h}{u}", tag=f"yb{2 * h + u}")
+                bbank[h, u] = bank
+                for e in range(2):
+                    cols = slice(C + (2 * u + e) * P, C + (2 * u + e + 1) * P)
+                    nc.tensor.matmul_mx(
+                        out=bank[:, e, :], lhsT=cwd[:, cols].bitcast(FP8X4), lhsT_scale=csd[:, cols],
+                        rhs=z2w[h][:].bitcast(FP8X4), rhs_scale=z2s[h][:], start=True, stop=True,
+                    )
+
+        for t in range(PACK):
+            nc.scalar.activation(y5[1][:, t, :], yc[t][:].indirect(half_list(l_n5, 1)), ACT.Copy)
+        z2_first(0)
+        nc.vector.quantize_mx(out=zw[:].bitcast(FP8X4), scales=zs[:], in_=zb[:])
+
+        a = [keep.tile([P, S], F32, name=f"a{t}") for t in range(PACK)]
+        b = [keep.tile([P, S], F32, name=f"b{t}") for t in range(PACK)]
+        a7 = [keep.tile([P, PACK, HALF], F32, name=f"a7_{h}") for h in range(2)]
+        for t in range(PACK):
+            cols = slice(t * P, (t + 1) * P)
+            bank = psum.tile([P, S], F32, name=f"abank{t}", tag=f"ab{t}")
+            nc.tensor.matmul_mx(
+                out=bank[:], lhsT=cwd[:, cols].bitcast(FP8X4), lhsT_scale=csd[:, cols],
+                rhs=zw[:].bitcast(FP8X4), rhs_scale=zs[:], start=True, stop=True,
+            )
+            nc.scalar.activation(a[t][:], bank[:], ACT.Copy, scale=0.75 * 0.0625 * 0.0625)
+        z2_second(0)
+        z2_first(1)
+        z2_matmul(0)
+        for h in range(2):
+            for t in range(PACK):
+                nc.scalar.activation(a7[h][:, t, :], a[t][:].indirect(half_list(l_n7, h)), ACT.Copy)
+        z2_second(1)
+        z2_matmul(1)
+
+        QUART = S // 4
+        m7 = [keep.tile([P, PACK, HALF], F32, name=f"m7_{h}") for h in range(2)]
+        m8 = [keep.tile([P, PACK, HALF], F32, name=f"m8_{h}") for h in range(2)]
+        b8 = keep.tile([P, PACK, HALF], F32, name="b8")
+        osc = keep.tile([P, S], U8, name="osc", align_bytes=64)
+        out_rows = out_0.rearrange("(p t) s -> p t s", t=PACK)
+        out_words = out_1[0].rearrange("p n t -> p (n t)").bitcast(I32)
+        for h in range(2):
+            for u in range(2):
+                nc.vector.tensor_tensor(m7[h][:, 2 * u : 2 * u + 2, :], a7[h][:, 2 * u : 2 * u + 2, :], bbank[h, u][:], MULT)
+            for t in range(PACK):
+                nc.scalar.copy(b[t][:, half_cols(h)], bbank[h, t // 2][:, t % 2, :])
+        for t in range(PACK):
+            nc.vector.tensor_tensor(m8[0][:, t, :], b[t][:].indirect(half_list(l_n8, 0)), a[t][:, half_cols(0)], MULT)
+            nc.scalar.activation(b8[:, t, :], b[t][:].indirect(half_list(l_n8, 1)), ACT.Copy)
+
+        def finish(name, h, lo, width):
+            cols = slice(h * HALF + lo, h * HALF + lo + width)
+            of = keep.tile([P, PACK, width], F32, name="of" + name)
+            ob = keep.tile([P, width * PACK], BF16, name="ob" + name, align_bytes=64)
+            nc.vector.tensor_tensor(of[:], m8[h][:, :, lo : lo + width], m7[h][:, :, lo : lo + width], SUB)
+            nc.sync.dma_start(out_rows[:, :, cols], of[:])
+            nc.scalar.copy(woven(ob[:]), planar(of[:]))
+            return name, cols, width, ob
+
+        def planes(name, cols, width, ob):
+            ow = keep.tile([P, width], U32, name="ow" + name, align_bytes=64)
+            nc.vector.quantize_mx(out=ow[:].bitcast(FP8X4), scales=osc[:, cols], in_=ob[:])
+            nc.sync.dma_start(out_words[:, cols], ow[:].bitcast(I32))
+
+        first = finish("a", 0, 0, HALF)
+        for t in range(PACK):
+            nc.vector.tensor_tensor(m8[1][:, t, :], b8[:, t, :], a[t][:, half_cols(1)], MULT)
+        second = finish("b", 1, 0, QUART)
+        planes(*first)
+        third = finish("c", 1, QUART, QUART)
+        planes(*second)
+        planes(*third)
+        for q in range(4):
+            nc.sync.dma_start(out_2[0, 4 * q : 4 * q + 4, :].bitcast(I32), osc[32 * q : 32 * q + 4, :].bitcast(I32))

@@ -38,8 +38,8 @@ def tile_picked_twocdcrossbrmsdet_none_po_kernel(
             nc.sync.dma_start(tile[:], src)
             return tile
 
-        def load_scales(engine, tile, src):
-            for q in range(4):
+        def load_scales(engines, tile, src):
+            for q, engine in enumerate(engines):
                 rows = src[0, 4 * q : 4 * q + 4, :].bitcast(I32)
                 engine.dma_start(tile[32 * q : 32 * q + 32, :].bitcast(I32), rows.partition_broadcast(8))
 
@@ -65,12 +65,12 @@ def tile_picked_twocdcrossbrmsdet_none_po_kernel(
         xw = keep.tile([P, T], U32, name="xw", align_bytes=64)
         ww = keep.tile([P, H], U32, name="ww", align_bytes=64)
         ws = keep.tile([P, H], U8, name="ws", align_bytes=64)
-        load_scales(nc.sync, xs, x_scales)
+        load_scales([nc.sync] * 4, xs, x_scales)
         l_offs = load_list("offs", offs)
         nc.sync.dma_start(ww[:].bitcast(I32), w1_words[0].rearrange("p n t -> p (n t)").bitcast(I32))
         nc.sync.dma_start(xw[:].bitcast(I32), x_words[0].rearrange("p n t -> p (n t)").bitcast(I32))
+        load_scales([nc.sync] + [nc.gpsimd] * 3, ws, w1_scales)
         l_ca = load_list("ca", ca)
-        load_scales(nc.sync, ws, w1_scales)
         l_cb = load_list("cb", cb)
         g1 = keep.tile([P, PACK], F32, name="g1")
         g2raw = keep.tile([P, PACK], F32, name="g2raw")
@@ -112,18 +112,21 @@ def tile_picked_twocdcrossbrmsdet_none_po_kernel(
         y = [keep.tile([P, S], F32, name=f"y{t}") for t in range(PACK)]
         yc = [keep.tile([P, S], F32, name=f"yc{t}") for t in range(PACK)]
         sq2 = [keep.tile([P, S], F32, name=f"sq2_{t}") for t in range(PACK)]
+        ybank = []
         for t in range(PACK):
             cols = slice(t * P, (t + 1) * P)
             bank = psum.tile([P, S], F32, name=f"ybank{t}", tag=f"yb{t}")
+            ybank.append(bank)
             nc.tensor.matmul_mx(
                 out=bank[:], lhsT=wwd[:, cols].bitcast(FP8X4), lhsT_scale=wsd[:, cols],
                 rhs=qw[:].bitcast(FP8X4), rhs_scale=qs[:], start=True, stop=True,
             )
             nc.scalar.activation(sq[t][:, :S], bank[:], ACT.Square)
             nc.sync.dma_start(sq2[t][:], sq[t][:, :S])
-            nc.scalar.copy(y[t][:], bank[:])
-            nc.gpsimd.tensor_scalar(yc[t][:], y[t][:], g2[:, t : t + 1], 0.0, MULT, ADD)
-            nc.gpsimd.tensor_scalar(yg[t][:, :S], y[t][:], g1[:, t : t + 1], 0.0, MULT, ADD)
+        for t in range(PACK):
+            nc.scalar.copy(y[t][:], ybank[t][:])
+        for t in range(PACK):
+            nc.scalar.activation(yc[t][:], ybank[t][:], ACT.Copy, scale=g2[:, t : t + 1])
 
         csb = keep.tile([P, C], U8, name="csb", tag="bytes0", align_bytes=64)
         nc.vector.tensor_copy(csb[:], xs[:].indirect(l_cb[:]))
@@ -138,17 +141,18 @@ def tile_picked_twocdcrossbrmsdet_none_po_kernel(
         y5 = [keep.tile([P, PACK, HALF], F32, name=f"y5_{h}") for h in range(2)]
         for t in range(PACK):
             nc.vector.tensor_tensor(ssum[t][:], sq[t][:].indirect(l_n1[:]), sq2[t][:], ADD)
-            nc.scalar.activation(y3[0][:, t, :], yc[t][:].indirect(half_list(l_n3, 0)), ACT.Copy)
+            nc.vector.tensor_scalar(yg[t][:, :S], y[t][:], g1[:, t : t + 1], None, MULT)
             nc.scalar.activation(rs[t][:], ssum[t][:], ACT.Abs_reciprocal_sqrt, bias=0.25)
+            nc.scalar.activation(y3[0][:, t, :], yc[t][:].indirect(half_list(l_n3, 0)), ACT.Copy)
         for t in range(PACK):
             nc.vector.tensor_tensor(zf[:, t, :], yg[t][:].indirect(l_n2[:]), rs[t][:], MULT)
             nc.scalar.activation(y5[0][:, t, :], yc[t][:].indirect(half_list(l_n5, 0)), ACT.Copy)
         zb = keep.tile([P, S * PACK], BF16, name="zb", align_bytes=64)
         zw = keep.tile([P, S], U32, name="zw", align_bytes=64)
         zs = keep.tile([P, S], U8, name="zs", align_bytes=64)
-        nc.scalar.copy(woven(zb[:]), planar(zf[:]))
         for t in range(PACK):
             nc.scalar.activation(y3[1][:, t, :], yc[t][:].indirect(half_list(l_n3, 1)), ACT.Copy)
+        nc.scalar.copy(woven(zb[:]), planar(zf[:]))
 
         p4 = [keep.tile([P, PACK, HALF], F32, name=f"p4_{h}") for h in range(2)]
         p6 = [keep.tile([P, PACK, HALF], F32, name=f"p6_{h}") for h in range(2)]

@@ -64,13 +64,13 @@ def tile_picked_twocdcrossbrmsdet_none_po_kernel(
         xs = keep.tile([P, T], U8, name="xs", align_bytes=64)
         xw = keep.tile([P, T], U32, name="xw", align_bytes=64)
         ww = keep.tile([P, H], U32, name="ww", align_bytes=64)
-        ws = keep.tile([P, H], U8, name="ws", align_bytes=64)
+        ws = keep.tile([P, H], U8, name="ws", tag="staged", align_bytes=64)
         load_scales([nc.sync] * 4, xs, x_scales)
         l_offs = load_list("offs", offs)
+        l_ca = load_list("ca", ca)
         nc.sync.dma_start(ww[:].bitcast(I32), w1_words[0].rearrange("p n t -> p (n t)").bitcast(I32))
         nc.sync.dma_start(xw[:].bitcast(I32), x_words[0].rearrange("p n t -> p (n t)").bitcast(I32))
         load_scales([nc.sync] + [nc.gpsimd] * 3, ws, w1_scales)
-        l_ca = load_list("ca", ca)
         l_cb = load_list("cb", cb)
         g1 = keep.tile([P, PACK], F32, name="g1")
         g2raw = keep.tile([P, PACK], F32, name="g2raw")
@@ -90,11 +90,13 @@ def tile_picked_twocdcrossbrmsdet_none_po_kernel(
         for t in range(PACK):
             nc.gpsimd.memset(sq[t][:, S:], 0.0)
             nc.gpsimd.memset(yg[t][:, S:], 0.0)
+        warm = keep.tile([P, 2], F32, name="warm")
+        nc.vector.memset(warm[:, 0:1], 1.0)
+        nc.scalar.activation(warm[:, 1:2], warm[:, 0:1], ACT.Abs_reciprocal_sqrt)
 
         qw = keep.tile([P, S], U32, name="qw", align_bytes=64)
-        qs = keep.tile([P, S], U8, name="qs", tag="bytes0", align_bytes=64)
-        cw = keep.tile([P, 2 * C], U32, name="cw", align_bytes=64)
-        csa = keep.tile([P, C], U8, name="csa", align_bytes=64)
+        qs = keep.tile([P, S], U8, name="qs", align_bytes=64)
+        cs = keep.tile([P, 2 * C], U8, name="cs", align_bytes=64)
         wwd = keep.tile([P, H], U32, name="wwd", align_bytes=64)
         wsd = keep.tile([P, H], U8, name="wsd", align_bytes=64)
         cwd = keep.tile([P, 2 * C], U32, name="cwd", align_bytes=64)
@@ -102,16 +104,14 @@ def tile_picked_twocdcrossbrmsdet_none_po_kernel(
         nc.vector.tensor_copy(qs[:], xs[:].indirect(l_offs[:]))
         deal(wwd[:], ww[:], 4)
         nc.vector.tensor_copy(qw[:], xw[:].indirect(l_offs[:]))
+        nc.vector.tensor_copy(cs[:, :C], xs[:].indirect(l_ca[:]))
         deal(wsd[:], ws[:], 16)
-        nc.vector.tensor_copy(csa[:], xs[:].indirect(l_ca[:]))
         g2 = keep.tile([P, PACK], F32, name="g2")
         nc.gpsimd.tensor_scalar(g2[:], g2raw[:], 0.75, 0.0, MULT, ADD)
-        nc.vector.tensor_copy(cw[:, :C], xw[:].indirect(l_ca[:]))
-        nc.vector.tensor_copy(cw[:, C:], xw[:].indirect(l_cb[:]))
 
-        y = [keep.tile([P, S], F32, name=f"y{t}") for t in range(PACK)]
-        yc = [keep.tile([P, S], F32, name=f"yc{t}") for t in range(PACK)]
-        sq2 = [keep.tile([P, S], F32, name=f"sq2_{t}") for t in range(PACK)]
+        y = [keep.tile([P, 2 * S], F32, name=f"y{t}") for t in range(PACK)]
+        yc = [keep.tile([P, 2 * S], F32, name=f"yc{t}") for t in range(PACK)]
+        a = [keep.tile([P, 2 * S], F32, name=f"a{t}") for t in range(PACK)]
         ybank = []
         for t in range(PACK):
             cols = slice(t * P, (t + 1) * P)
@@ -122,53 +122,64 @@ def tile_picked_twocdcrossbrmsdet_none_po_kernel(
                 rhs=qw[:].bitcast(FP8X4), rhs_scale=qs[:], start=True, stop=True,
             )
             nc.scalar.activation(sq[t][:, :S], bank[:], ACT.Square)
-            nc.sync.dma_start(sq2[t][:], sq[t][:, :S])
+            nc.sync.dma_start(yc[t][:, S:], sq[t][:, :S])
         for t in range(PACK):
-            nc.scalar.copy(y[t][:], ybank[t][:])
-        for t in range(PACK):
-            nc.scalar.activation(yc[t][:], ybank[t][:], ACT.Copy, scale=g2[:, t : t + 1])
+            nc.scalar.copy(y[t][:, :S], ybank[t][:])
 
-        csb = keep.tile([P, C], U8, name="csb", tag="bytes0", align_bytes=64)
-        nc.vector.tensor_copy(csb[:], xs[:].indirect(l_cb[:]))
+        cw = keep.tile([P, 2 * C], U32, name="cw", tag="staged", align_bytes=64)
+        nc.vector.tensor_copy(cw[:, :C], xw[:].indirect(l_ca[:]))
+        nc.vector.tensor_copy(cw[:, C:], xw[:].indirect(l_cb[:]))
+
+        rs = keep.tile([P, PACK, S], F32, name="rs")
+        y2 = keep.tile([P, PACK, S], F32, name="yn2")
+        y5 = keep.tile([P, PACK, S], F32, name="yn5")
+        p4 = keep.tile([P, PACK, S], F32, name="p4")
+        for t in range(PACK):
+            nc.vector.tensor_scalar(yg[t][:, :S], y[t][:, :S], g1[:, t : t + 1], None, MULT)
+        for t in range(PACK):
+            nc.vector.tensor_scalar(yc[t][:, :S], y[t][:, :S], g2[:, t : t + 1], None, MULT)
+        nc.vector.tensor_copy(cs[:, C:], xs[:].indirect(l_cb[:]))
+        for t in range(PACK):
+            nc.vector.tensor_tensor(y[t][:, S:], sq[t][:].indirect(l_n1[:]), yc[t][:, S:], ADD)
+        for t in range(PACK):
+            nc.scalar.activation(y2[:, t, :], yg[t][:].indirect(l_n2[:]), ACT.Copy)
+        for t in range(PACK):
+            nc.scalar.activation(rs[:, t, :], y[t][:, S:], ACT.Abs_reciprocal_sqrt, bias=0.25)
+        for t in range(PACK):
+            nc.scalar.activation(a[t][:, S:], yc[t][:].indirect(l_n3[:]), ACT.Copy)
+        for t in range(PACK):
+            nc.scalar.activation(y5[:, t, :], yc[t][:].indirect(l_n5[:]), ACT.Copy)
         deal(cwd[:], cw[:], 4)
-        deal(csd[:, :C], csa[:], 16)
-        deal(csd[:, C:], csb[:], 16)
-
-        ssum = [keep.tile([P, S], F32, name=f"ssum{t}") for t in range(PACK)]
-        rs = [keep.tile([P, S], F32, name=f"rs{t}") for t in range(PACK)]
-        zf = keep.tile([P, PACK, S], F32, name="zf")
-        y3 = [keep.tile([P, PACK, HALF], F32, name=f"y3_{h}") for h in range(2)]
-        y5 = [keep.tile([P, PACK, HALF], F32, name=f"y5_{h}") for h in range(2)]
-        for t in range(PACK):
-            nc.vector.tensor_tensor(ssum[t][:], sq[t][:].indirect(l_n1[:]), sq2[t][:], ADD)
-            nc.vector.tensor_scalar(yg[t][:, :S], y[t][:], g1[:, t : t + 1], None, MULT)
-            nc.scalar.activation(rs[t][:], ssum[t][:], ACT.Abs_reciprocal_sqrt, bias=0.25)
-            nc.scalar.activation(y3[0][:, t, :], yc[t][:].indirect(half_list(l_n3, 0)), ACT.Copy)
-        for t in range(PACK):
-            nc.vector.tensor_tensor(zf[:, t, :], yg[t][:].indirect(l_n2[:]), rs[t][:], MULT)
-            nc.scalar.activation(y5[0][:, t, :], yc[t][:].indirect(half_list(l_n5, 0)), ACT.Copy)
+        deal(csd[:], cs[:], 16)
         zb = keep.tile([P, S * PACK], BF16, name="zb", align_bytes=64)
         zw = keep.tile([P, S], U32, name="zw", align_bytes=64)
         zs = keep.tile([P, S], U8, name="zs", align_bytes=64)
-        for t in range(PACK):
-            nc.scalar.activation(y3[1][:, t, :], yc[t][:].indirect(half_list(l_n3, 1)), ACT.Copy)
-        nc.scalar.copy(woven(zb[:]), planar(zf[:]))
+        nc.vector.tensor_tensor(woven(zb[:]), planar(y2[:]), planar(rs[:]), MULT)
+        nc.vector.quantize_mx(out=zw[:].bitcast(FP8X4), scales=zs[:], in_=zb[:])
 
-        p4 = [keep.tile([P, PACK, HALF], F32, name=f"p4_{h}") for h in range(2)]
-        p6 = [keep.tile([P, PACK, HALF], F32, name=f"p6_{h}") for h in range(2)]
+        b = [keep.tile([P, S], F32, name=f"b{t}") for t in range(PACK)]
+        a7 = keep.tile([P, PACK, S], F32, name="an7")
+        for t in range(PACK):
+            cols = slice(t * P, (t + 1) * P)
+            bank = psum.tile([P, S], F32, name=f"abank{t}", tag=f"ab{t}")
+            nc.tensor.matmul_mx(
+                out=bank[:], lhsT=cwd[:, cols].bitcast(FP8X4), lhsT_scale=csd[:, cols],
+                rhs=zw[:].bitcast(FP8X4), rhs_scale=zs[:], start=True, stop=True,
+            )
+            nc.scalar.activation(a[t][:, :S], bank[:], ACT.Copy, scale=0.75 * 0.0625 * 0.0625)
+
+        p6 = keep.tile([P, PACK, S], F32, name="p6")
         z2b = [keep.tile([P, HALF * PACK], BF16, name=f"z2b{h}", align_bytes=64) for h in range(2)]
         z2w = [keep.tile([P, HALF], U32, name=f"z2w{h}", align_bytes=64) for h in range(2)]
         z2s = [keep.tile([P, HALF], U8, name=f"z2s{h}", align_bytes=64) for h in range(2)]
         bbank = {}
 
-        def z2_first(h):
-            for t in range(PACK):
-                nc.vector.tensor_tensor(p4[h][:, t, :], y[t][:].indirect(half_list(l_n4, h)), y3[h][:, t, :], MULT)
-
         def z2_second(h):
             for t in range(PACK):
-                nc.vector.tensor_tensor(p6[h][:, t, :], y[t][:].indirect(half_list(l_n6, h)), y5[h][:, t, :], MULT)
-            nc.vector.tensor_tensor(woven(z2b[h][:]), planar(p4[h][:]), planar(p6[h][:]), SUB)
+                nc.vector.tensor_tensor(p6[:, t, half_cols(h)], y[t][:].indirect(half_list(l_n6, h)), y5[:, t, half_cols(h)], MULT)
+
+        def z2_round(h):
+            nc.vector.tensor_tensor(woven(z2b[h][:]), planar(p4[:, :, half_cols(h)]), planar(p6[:, :, half_cols(h)]), SUB)
 
         def z2_matmul(h):
             nc.vector.quantize_mx(out=z2w[h][:].bitcast(FP8X4), scales=z2s[h][:], in_=z2b[h][:])
@@ -182,54 +193,68 @@ def tile_picked_twocdcrossbrmsdet_none_po_kernel(
                         rhs=z2w[h][:].bitcast(FP8X4), rhs_scale=z2s[h][:], start=True, stop=True,
                     )
 
-        for t in range(PACK):
-            nc.scalar.activation(y5[1][:, t, :], yc[t][:].indirect(half_list(l_n5, 1)), ACT.Copy)
-        z2_first(0)
-        nc.vector.quantize_mx(out=zw[:].bitcast(FP8X4), scales=zs[:], in_=zb[:])
+        def gather_a(t):
+            nc.scalar.activation(a7[:, t, :], a[t][:].indirect(l_n7[:]), ACT.Copy)
 
-        a = [keep.tile([P, S], F32, name=f"a{t}") for t in range(PACK)]
-        b = [keep.tile([P, S], F32, name=f"b{t}") for t in range(PACK)]
-        a7 = [keep.tile([P, PACK, HALF], F32, name=f"a7_{h}") for h in range(2)]
-        for t in range(PACK):
-            cols = slice(t * P, (t + 1) * P)
-            bank = psum.tile([P, S], F32, name=f"abank{t}", tag=f"ab{t}")
-            nc.tensor.matmul_mx(
-                out=bank[:], lhsT=cwd[:, cols].bitcast(FP8X4), lhsT_scale=csd[:, cols],
-                rhs=zw[:].bitcast(FP8X4), rhs_scale=zs[:], start=True, stop=True,
-            )
-            nc.scalar.activation(a[t][:], bank[:], ACT.Copy, scale=0.75 * 0.0625 * 0.0625)
-        z2_second(0)
-        z2_first(1)
-        z2_matmul(0)
-        for h in range(2):
+        def copy_b(h):
             for t in range(PACK):
-                nc.scalar.activation(a7[h][:, t, :], a[t][:].indirect(half_list(l_n7, h)), ACT.Copy)
+                nc.scalar.copy(b[t][:, half_cols(h)], bbank[h, t // 2][:, t % 2, :])
+
+        for t in range(PACK):
+            nc.vector.tensor_tensor(p4[:, t, :], y[t][:].indirect(l_n4[:]), a[t][:, S:], MULT)
+        z2_second(0)
+        z2_round(0)
+        gather_a(0)
+        gather_a(1)
         z2_second(1)
+        z2_matmul(0)
+        copy_b(0)
+        z2_round(1)
         z2_matmul(1)
+        copy_b(1)
+        gather_a(2)
+        gather_a(3)
 
         QUART = S // 4
         m7 = [keep.tile([P, PACK, HALF], F32, name=f"m7_{h}") for h in range(2)]
         m8 = [keep.tile([P, PACK, HALF], F32, name=f"m8_{h}") for h in range(2)]
-        b8 = keep.tile([P, PACK, HALF], F32, name="b8")
+        b8 = [keep.tile([P, PACK, HALF], F32, name=f"bn8_{h}") for h in range(2)]
         osc = keep.tile([P, S], U8, name="osc", align_bytes=64)
         out_rows = out_0.rearrange("(p t) s -> p t s", t=PACK)
         out_words = out_1[0].rearrange("p n t -> p (n t)").bitcast(I32)
-        for h in range(2):
-            for u in range(2):
-                nc.vector.tensor_tensor(m7[h][:, 2 * u : 2 * u + 2, :], a7[h][:, 2 * u : 2 * u + 2, :], bbank[h, u][:], MULT)
-            for t in range(PACK):
-                nc.scalar.copy(b[t][:, half_cols(h)], bbank[h, t // 2][:, t % 2, :])
-        for t in range(PACK):
-            nc.vector.tensor_tensor(m8[0][:, t, :], b[t][:].indirect(half_list(l_n8, 0)), a[t][:, half_cols(0)], MULT)
-            nc.scalar.activation(b8[:, t, :], b[t][:].indirect(half_list(l_n8, 1)), ACT.Copy)
 
-        def finish(name, h, lo, width):
+        def times_b(h, u):
+            ts = slice(2 * u, 2 * u + 2)
+            nc.vector.tensor_tensor(m7[h][:, ts, :], a7[:, ts, half_cols(h)], bbank[h, u][:], MULT)
+
+        times_b(0, 0)
+        times_b(1, 0)
+        FUSED = 1
+
+        def gather_b(h, t):
+            nc.scalar.activation(b8[h][:, t, :], b[t][:].indirect(half_list(l_n8, h)), ACT.Copy)
+
+        def times_a(h, t):
+            nc.vector.tensor_tensor(m8[h][:, t, :], b8[h][:, t, :], a[t][:, half_cols(h)], MULT)
+
+        for t in range(FUSED, PACK):
+            gather_b(0, t)
+        for t in range(PACK):
+            gather_b(1, t)
+        for t in range(FUSED):
+            nc.vector.tensor_tensor(m8[0][:, t, :], b[t][:].indirect(half_list(l_n8, 0)), a[t][:, half_cols(0)], MULT)
+        times_b(0, 1)
+        times_b(1, 1)
+        for t in range(FUSED, PACK):
+            times_a(0, t)
+
+        def finish(name, h, lo, width, weave):
             cols = slice(h * HALF + lo, h * HALF + lo + width)
             of = keep.tile([P, PACK, width], F32, name="of" + name)
             ob = keep.tile([P, width * PACK], BF16, name="ob" + name, align_bytes=64)
             nc.vector.tensor_tensor(of[:], m8[h][:, :, lo : lo + width], m7[h][:, :, lo : lo + width], SUB)
             nc.sync.dma_start(out_rows[:, :, cols], of[:])
-            nc.scalar.copy(woven(ob[:]), planar(of[:]))
+            weave(woven(ob[:]), planar(of[:]))
             return name, cols, width, ob
 
         def planes(name, cols, width, ob):
@@ -237,12 +262,12 @@ def tile_picked_twocdcrossbrmsdet_none_po_kernel(
             nc.vector.quantize_mx(out=ow[:].bitcast(FP8X4), scales=osc[:, cols], in_=ob[:])
             nc.sync.dma_start(out_words[:, cols], ow[:].bitcast(I32))
 
-        first = finish("a", 0, 0, HALF)
+        first = finish("a", 0, 0, HALF, nc.scalar.copy)
         for t in range(PACK):
-            nc.vector.tensor_tensor(m8[1][:, t, :], b8[:, t, :], a[t][:, half_cols(1)], MULT)
-        second = finish("b", 1, 0, QUART)
+            times_a(1, t)
+        second = finish("b", 1, 0, QUART, nc.scalar.copy)
         planes(*first)
-        third = finish("c", 1, QUART, QUART)
+        third = finish("c", 1, QUART, QUART, nc.vector.tensor_copy)
         planes(*second)
         planes(*third)
         for q in range(4):

@@ -19,9 +19,15 @@ SUB = mybir.AluOpType.subtract
 
 P = 128
 PACK = 4
+QUADS = 4
 HALF = S // 2
+QUART = S // 4
+LIST_COLS = S // 16
 SPARE = 16
-LCOL = S // 16
+WORD_RUN = 4
+BYTE_RUN = 16
+OUT_SCALE = 0.75 * 0.0625 * 0.0625
+FUSED_N8 = 3
 
 
 def tile_picked_twocdcrossbrmsdet_none_po_kernel(
@@ -29,25 +35,30 @@ def tile_picked_twocdcrossbrmsdet_none_po_kernel(
     out_0, out_1, out_2,
 ):
     nc = tc.nc
+    planes = range(PACK)
+    halves = range(2)
     with ExitStack() as ctx:
         keep = ctx.enter_context(tc.tile_pool(name="keep", bufs=1))
         psum = ctx.enter_context(tc.psum_pool(name="psum", bufs=1))
 
         def load_list(name, src):
-            tile = keep.tile([P, LCOL], U16, name="list_" + name)
+            tile = keep.tile([P, LIST_COLS], U16, name="list_" + name)
             nc.sync.dma_start(tile[:], src)
             return tile
 
-        def load_scales(engines, tile, src):
-            for q, engine in enumerate(engines):
+        def load_scales(queues, tile, src):
+            for q, queue in enumerate(queues):
                 rows = src[0, 4 * q : 4 * q + 4, :].bitcast(I32)
-                engine.dma_start(tile[32 * q : 32 * q + 32, :].bitcast(I32), rows.partition_broadcast(8))
+                queue.dma_start(tile[32 * q : 32 * q + 32, :].bitcast(I32), rows.partition_broadcast(8))
+
+        def as_words(dram):
+            return dram[0].rearrange("p n t -> p (n t)").bitcast(I32)
 
         def half_cols(h):
             return slice(h * HALF, (h + 1) * HALF)
 
         def half_list(lst, h):
-            return lst[:, h * (LCOL // 2) : (h + 1) * (LCOL // 2)]
+            return lst[:, h * (LIST_COLS // 2) : (h + 1) * (LIST_COLS // 2)]
 
         def deal(dst, src, run):
             nc.vector.tensor_copy(
@@ -56,26 +67,32 @@ def tile_picked_twocdcrossbrmsdet_none_po_kernel(
             )
 
         def woven(ap):
-            return ap.rearrange("p (c i t) -> p c t i", i=4, t=PACK)
+            return ap.rearrange("p (c i t) -> p c t i", i=WORD_RUN, t=PACK)
 
         def planar(ap):
-            return ap.rearrange("p t (c i) -> p c t i", i=4)
+            return ap.rearrange("p t (c i) -> p c t i", i=WORD_RUN)
 
-        xs = keep.tile([P, T], U8, name="xs", align_bytes=64)
-        xw = keep.tile([P, T], U32, name="xw", align_bytes=64)
-        ww = keep.tile([P, H], U32, name="ww", align_bytes=64)
-        ws = keep.tile([P, H], U8, name="ws", tag="staged", align_bytes=64)
-        load_scales([nc.sync] * 4, xs, x_scales)
+        def mx_pass(out, lhs_words, lhs_scales, cols, rhs_words, rhs_scales):
+            nc.tensor.matmul_mx(
+                out=out, lhsT=lhs_words[:, cols].bitcast(FP8X4), lhsT_scale=lhs_scales[:, cols],
+                rhs=rhs_words[:].bitcast(FP8X4), rhs_scale=rhs_scales[:], start=True, stop=True,
+            )
+
+        x_s = keep.tile([P, T], U8, name="x_s", align_bytes=64)
+        x_w = keep.tile([P, T], U32, name="x_w", align_bytes=64)
+        w_w = keep.tile([P, H], U32, name="w_w", align_bytes=64)
+        w_s = keep.tile([P, H], U8, name="w_s", tag="staged", align_bytes=64)
+        load_scales([nc.sync] * QUADS, x_s, x_scales)
         l_offs = load_list("offs", offs)
         l_ca = load_list("ca", ca)
-        nc.sync.dma_start(ww[:].bitcast(I32), w1_words[0].rearrange("p n t -> p (n t)").bitcast(I32))
-        nc.sync.dma_start(xw[:].bitcast(I32), x_words[0].rearrange("p n t -> p (n t)").bitcast(I32))
-        load_scales([nc.sync] + [nc.gpsimd] * 3, ws, w1_scales)
+        nc.sync.dma_start(w_w[:].bitcast(I32), as_words(w1_words))
+        nc.sync.dma_start(x_w[:].bitcast(I32), as_words(x_words))
+        load_scales([nc.sync] + [nc.gpsimd] * (QUADS - 1), w_s, w1_scales)
         l_cb = load_list("cb", cb)
-        g1 = keep.tile([P, PACK], F32, name="g1")
-        g2raw = keep.tile([P, PACK], F32, name="g2raw")
-        nc.sync.dma_start(g1[:], gs.rearrange("(p t) o -> p (t o)", t=PACK))
-        nc.sync.dma_start(g2raw[:], gs2.rearrange("(p t) o -> p (t o)", t=PACK))
+        gain_z = keep.tile([P, PACK], F32, name="gain_z")
+        gain_z2_in = keep.tile([P, PACK], F32, name="gain_z2_in")
+        nc.sync.dma_start(gain_z[:], gs.rearrange("(p t) o -> p (t o)", t=PACK))
+        nc.sync.dma_start(gain_z2_in[:], gs2.rearrange("(p t) o -> p (t o)", t=PACK))
         l_n1 = load_list("n1", n1)
         l_n3 = load_list("n3", n3)
         l_n5 = load_list("n5", n5)
@@ -85,190 +102,176 @@ def tile_picked_twocdcrossbrmsdet_none_po_kernel(
         l_n7 = load_list("n7", n7)
         l_n8 = load_list("n8", n8)
 
-        sq = [keep.tile([P, S + SPARE], F32, name=f"sq{t}") for t in range(PACK)]
-        yg = [keep.tile([P, S + SPARE], F32, name=f"yg{t}") for t in range(PACK)]
-        for t in range(PACK):
+        sq = [keep.tile([P, S + SPARE], F32, name=f"sq{t}", align_bytes=64) for t in planes]
+        y_gs = [keep.tile([P, S + SPARE], F32, name=f"y_gs{t}") for t in planes]
+        for t in planes:
             nc.gpsimd.memset(sq[t][:, S:], 0.0)
-            nc.gpsimd.memset(yg[t][:, S:], 0.0)
+            nc.gpsimd.memset(y_gs[t][:, S:], 0.0)
+
         warm = keep.tile([P, 2], F32, name="warm")
         nc.vector.memset(warm[:, 0:1], 1.0)
         nc.scalar.activation(warm[:, 1:2], warm[:, 0:1], ACT.Abs_reciprocal_sqrt)
 
-        qw = keep.tile([P, S], U32, name="qw", align_bytes=64)
-        qs = keep.tile([P, S], U8, name="qs", align_bytes=64)
-        cs = keep.tile([P, 2 * C], U8, name="cs", align_bytes=64)
-        wwd = keep.tile([P, H], U32, name="wwd", align_bytes=64)
-        wsd = keep.tile([P, H], U8, name="wsd", align_bytes=64)
-        cwd = keep.tile([P, 2 * C], U32, name="cwd", align_bytes=64)
-        csd = keep.tile([P, 2 * C], U8, name="csd", align_bytes=64)
-        nc.vector.tensor_copy(qs[:], xs[:].indirect(l_offs[:]))
-        deal(wwd[:], ww[:], 4)
-        nc.vector.tensor_copy(qw[:], xw[:].indirect(l_offs[:]))
-        nc.vector.tensor_copy(cs[:, :C], xs[:].indirect(l_ca[:]))
-        deal(wsd[:], ws[:], 16)
-        g2 = keep.tile([P, PACK], F32, name="g2")
-        nc.gpsimd.tensor_scalar(g2[:], g2raw[:], 0.75, 0.0, MULT, ADD)
+        q_w = keep.tile([P, S], U32, name="q_w", align_bytes=64)
+        q_s = keep.tile([P, S], U8, name="q_s", align_bytes=64)
+        c_s = keep.tile([P, 2 * C], U8, name="c_s", align_bytes=64)
+        w_w_dealt = keep.tile([P, H], U32, name="w_w_dealt", align_bytes=64)
+        w_s_dealt = keep.tile([P, H], U8, name="w_s_dealt", align_bytes=64)
+        nc.vector.tensor_copy(q_s[:], x_s[:].indirect(l_offs[:]))
+        deal(w_w_dealt[:], w_w[:], WORD_RUN)
+        nc.vector.tensor_copy(q_w[:], x_w[:].indirect(l_offs[:]))
+        nc.vector.tensor_copy(c_s[:, :C], x_s[:].indirect(l_ca[:]))
+        deal(w_s_dealt[:], w_s[:], BYTE_RUN)
+        gain_z2 = keep.tile([P, PACK], F32, name="gain_z2")
+        nc.gpsimd.tensor_scalar(gain_z2[:], gain_z2_in[:], 0.75, 0.0, MULT, ADD)
 
-        y = [keep.tile([P, 2 * S], F32, name=f"y{t}") for t in range(PACK)]
-        yc = [keep.tile([P, 2 * S], F32, name=f"yc{t}") for t in range(PACK)]
-        a = [keep.tile([P, 2 * S], F32, name=f"a{t}") for t in range(PACK)]
-        ybank = []
-        for t in range(PACK):
-            cols = slice(t * P, (t + 1) * P)
-            bank = psum.tile([P, S], F32, name=f"ybank{t}", tag=f"yb{t}")
-            ybank.append(bank)
-            nc.tensor.matmul_mx(
-                out=bank[:], lhsT=wwd[:, cols].bitcast(FP8X4), lhsT_scale=wsd[:, cols],
-                rhs=qw[:].bitcast(FP8X4), rhs_scale=qs[:], start=True, stop=True,
-            )
+        y = [keep.tile([P, S], F32, name=f"y{t}") for t in planes]
+        y_gs2 = [keep.tile([P, 2 * S], F32, name=f"y_gs2_{t}") for t in planes]
+        a = [keep.tile([P, S], F32, name=f"a{t}") for t in planes]
+        y_bank = []
+        for t in planes:
+            bank = psum.tile([P, S], F32, name=f"y_bank{t}", tag=f"yb_bank{t}")
+            y_bank.append(bank)
+            mx_pass(bank[:], w_w_dealt, w_s_dealt, slice(t * P, (t + 1) * P), q_w, q_s)
             nc.scalar.activation(sq[t][:, :S], bank[:], ACT.Square)
-            nc.sync.dma_start(yc[t][:, S:], sq[t][:, :S])
-        for t in range(PACK):
-            nc.scalar.copy(y[t][:, :S], ybank[t][:])
+            nc.sync.dma_start(y_gs2[t][:, S:], sq[t][:, :S])
+        for t in planes:
+            nc.scalar.copy(y[t][:], y_bank[t][:])
 
-        cw = keep.tile([P, 2 * C], U32, name="cw", tag="staged", align_bytes=64)
-        nc.vector.tensor_copy(cw[:, :C], xw[:].indirect(l_ca[:]))
-        nc.vector.tensor_copy(cw[:, C:], xw[:].indirect(l_cb[:]))
+        c_w = keep.tile([P, 2 * C], U32, name="c_w", tag="staged", align_bytes=64)
+        nc.vector.tensor_copy(c_w[:, :C], x_w[:].indirect(l_ca[:]))
+        nc.vector.tensor_copy(c_w[:, C:], x_w[:].indirect(l_cb[:]))
 
-        rs = keep.tile([P, PACK, S], F32, name="rs")
-        y2 = keep.tile([P, PACK, S], F32, name="yn2")
-        y5 = keep.tile([P, PACK, S], F32, name="yn5")
-        p4 = keep.tile([P, PACK, S], F32, name="p4")
-        for t in range(PACK):
-            nc.vector.tensor_scalar(yg[t][:, :S], y[t][:, :S], g1[:, t : t + 1], None, MULT)
-        for t in range(PACK):
-            nc.vector.tensor_scalar(yc[t][:, :S], y[t][:, :S], g2[:, t : t + 1], None, MULT)
-        nc.vector.tensor_copy(cs[:, C:], xs[:].indirect(l_cb[:]))
-        for t in range(PACK):
-            nc.vector.tensor_tensor(y[t][:, S:], sq[t][:].indirect(l_n1[:]), yc[t][:, S:], ADD)
-        for t in range(PACK):
-            nc.scalar.activation(y2[:, t, :], yg[t][:].indirect(l_n2[:]), ACT.Copy)
-        for t in range(PACK):
-            nc.scalar.activation(rs[:, t, :], y[t][:, S:], ACT.Abs_reciprocal_sqrt, bias=0.25)
-        for t in range(PACK):
-            nc.scalar.activation(a[t][:, S:], yc[t][:].indirect(l_n3[:]), ACT.Copy)
-        for t in range(PACK):
-            nc.scalar.activation(y5[:, t, :], yc[t][:].indirect(l_n5[:]), ACT.Copy)
-        deal(cwd[:], cw[:], 4)
-        deal(csd[:], cs[:], 16)
-        zb = keep.tile([P, S * PACK], BF16, name="zb", align_bytes=64)
-        zw = keep.tile([P, S], U32, name="zw", align_bytes=64)
-        zs = keep.tile([P, S], U8, name="zs", align_bytes=64)
-        nc.vector.tensor_tensor(woven(zb[:]), planar(y2[:]), planar(rs[:]), MULT)
-        nc.vector.quantize_mx(out=zw[:].bitcast(FP8X4), scales=zs[:], in_=zb[:])
+        inv_root = keep.tile([P, PACK, S], F32, name="inv_root")
+        y_n2 = keep.tile([P, PACK, S], F32, name="y_n2", tag="rows0")
+        sq_sum = keep.tile([P, PACK, S], F32, name="sq_sum", tag="rows1")
+        prod_34 = keep.tile([P, PACK, S], F32, name="prod_34")
+        for t in planes:
+            nc.vector.tensor_scalar(y_gs[t][:, :S], y[t][:], gain_z[:, t : t + 1], None, MULT)
+        for t in planes:
+            nc.vector.tensor_scalar(y_gs2[t][:, :S], y[t][:], gain_z2[:, t : t + 1], None, MULT)
+        nc.vector.tensor_copy(c_s[:, C:], x_s[:].indirect(l_cb[:]))
+        for t in planes:
+            nc.vector.tensor_tensor(sq_sum[:, t, :], sq[t][:].indirect(l_n1[:]), y_gs2[t][:, S:], ADD)
+        for t in planes:
+            nc.scalar.activation(y_n2[:, t, :], y_gs[t][:].indirect(l_n2[:]), ACT.Copy)
+        for t in planes:
+            nc.scalar.activation(inv_root[:, t, :], sq_sum[:, t, :], ACT.Abs_reciprocal_sqrt, bias=0.25)
 
-        b = [keep.tile([P, S], F32, name=f"b{t}") for t in range(PACK)]
-        a7 = keep.tile([P, PACK, S], F32, name="an7")
-        for t in range(PACK):
-            cols = slice(t * P, (t + 1) * P)
-            bank = psum.tile([P, S], F32, name=f"abank{t}", tag=f"ab{t}")
-            nc.tensor.matmul_mx(
-                out=bank[:], lhsT=cwd[:, cols].bitcast(FP8X4), lhsT_scale=csd[:, cols],
-                rhs=zw[:].bitcast(FP8X4), rhs_scale=zs[:], start=True, stop=True,
-            )
-            nc.scalar.activation(a[t][:, :S], bank[:], ACT.Copy, scale=0.75 * 0.0625 * 0.0625)
+        c_w_dealt = keep.tile([P, 2 * C], U32, name="c_w_dealt", tag=f"sq{PACK - 1}", align_bytes=64)
+        c_s_dealt = keep.tile([P, 2 * C], U8, name="c_s_dealt", tag=f"sq{PACK - 2}", align_bytes=64)
+        deal(c_w_dealt[:], c_w[:], WORD_RUN)
+        deal(c_s_dealt[:], c_s[:], BYTE_RUN)
+        z_bf = keep.tile([P, S * PACK], BF16, name="z_bf", align_bytes=64)
+        z_w = keep.tile([P, S], U32, name="z_w", align_bytes=64)
+        z_s = keep.tile([P, S], U8, name="z_s", align_bytes=64)
+        nc.vector.tensor_tensor(woven(z_bf[:]), planar(y_n2[:]), planar(inv_root[:]), MULT)
 
-        p6 = keep.tile([P, PACK, S], F32, name="p6")
-        z2b = [keep.tile([P, HALF * PACK], BF16, name=f"z2b{h}", align_bytes=64) for h in range(2)]
-        z2w = [keep.tile([P, HALF], U32, name=f"z2w{h}", align_bytes=64) for h in range(2)]
-        z2s = [keep.tile([P, HALF], U8, name=f"z2s{h}", align_bytes=64) for h in range(2)]
-        bbank = {}
+        y_n3 = keep.tile([P, PACK, S], F32, name="y_n3", tag="rows1")
+        y_n5 = keep.tile([P, PACK, S], F32, name="y_n5", tag="rows0")
+        for t in planes:
+            nc.scalar.activation(y_n3[:, t, :], y_gs2[t][:].indirect(l_n3[:]), ACT.Copy)
+        for t in planes:
+            nc.scalar.activation(y_n5[:, t, :], y_gs2[t][:].indirect(l_n5[:]), ACT.Copy)
+        nc.vector.quantize_mx(out=z_w[:].bitcast(FP8X4), scales=z_s[:], in_=z_bf[:])
 
-        def z2_second(h):
-            for t in range(PACK):
-                nc.vector.tensor_tensor(p6[:, t, half_cols(h)], y[t][:].indirect(half_list(l_n6, h)), y5[:, t, half_cols(h)], MULT)
+        b = [keep.tile([P, S], F32, name=f"b{t}") for t in planes]
+        a_n7 = keep.tile([P, PACK, S], F32, name="a_n7")
+        for t in planes:
+            bank = psum.tile([P, S], F32, name=f"a_bank{t}")
+            mx_pass(bank[:], c_w_dealt, c_s_dealt, slice(t * P, (t + 1) * P), z_w, z_s)
+            nc.scalar.activation(a[t][:], bank[:], ACT.Copy, scale=OUT_SCALE)
+
+        prod_56 = keep.tile([P, PACK, S], F32, name="prod_56")
+        z2_bf = [keep.tile([P, HALF * PACK], BF16, name=f"z2_bf{h}", align_bytes=64) for h in halves]
+        z2_w = [keep.tile([P, HALF], U32, name=f"z2_w{h}", align_bytes=64) for h in halves]
+        z2_s = [keep.tile([P, HALF], U8, name=f"z2_s{h}", align_bytes=64) for h in halves]
+        b_bank = {}
+
+        def gather_times(dst, window, lst, other, h):
+            nc.vector.tensor_tensor(dst, window[:].indirect(half_list(lst, h)), other, MULT)
+
+        def z2_second_product(h):
+            for t in planes:
+                gather_times(prod_56[:, t, half_cols(h)], y[t], l_n6, y_n5[:, t, half_cols(h)], h)
 
         def z2_round(h):
-            nc.vector.tensor_tensor(woven(z2b[h][:]), planar(p4[:, :, half_cols(h)]), planar(p6[:, :, half_cols(h)]), SUB)
+            cols = half_cols(h)
+            nc.vector.tensor_tensor(woven(z2_bf[h][:]), planar(prod_34[:, :, cols]), planar(prod_56[:, :, cols]), SUB)
 
-        def z2_matmul(h):
-            nc.vector.quantize_mx(out=z2w[h][:].bitcast(FP8X4), scales=z2s[h][:], in_=z2b[h][:])
+        def b_product(h):
+            nc.vector.quantize_mx(out=z2_w[h][:].bitcast(FP8X4), scales=z2_s[h][:], in_=z2_bf[h][:])
             for u in range(2):
-                bank = psum.tile([P, 2, HALF], F32, name=f"bbank{h}{u}", tag=f"yb{2 * h + u}")
-                bbank[h, u] = bank
+                bank = psum.tile([P, 2, HALF], F32, name=f"b_bank{h}{u}", tag=f"yb_bank{2 * h + u}")
+                b_bank[h, u] = bank
                 for e in range(2):
-                    cols = slice(C + (2 * u + e) * P, C + (2 * u + e + 1) * P)
-                    nc.tensor.matmul_mx(
-                        out=bank[:, e, :], lhsT=cwd[:, cols].bitcast(FP8X4), lhsT_scale=csd[:, cols],
-                        rhs=z2w[h][:].bitcast(FP8X4), rhs_scale=z2s[h][:], start=True, stop=True,
-                    )
+                    first_col = C + (2 * u + e) * P
+                    mx_pass(bank[:, e, :], c_w_dealt, c_s_dealt, slice(first_col, first_col + P), z2_w[h], z2_s[h])
 
-        def gather_a(t):
-            nc.scalar.activation(a7[:, t, :], a[t][:].indirect(l_n7[:]), ACT.Copy)
-
-        def copy_b(h):
-            for t in range(PACK):
-                nc.scalar.copy(b[t][:, half_cols(h)], bbank[h, t // 2][:, t % 2, :])
-
-        for t in range(PACK):
-            nc.vector.tensor_tensor(p4[:, t, :], y[t][:].indirect(l_n4[:]), a[t][:, S:], MULT)
-        z2_second(0)
+        for t in planes:
+            for h in halves:
+                gather_times(prod_34[:, t, half_cols(h)], y[t], l_n4, y_n3[:, t, half_cols(h)], h)
+        z2_second_product(0)
         z2_round(0)
-        gather_a(0)
-        gather_a(1)
-        z2_second(1)
-        z2_matmul(0)
-        copy_b(0)
+        for t in planes:
+            for h in halves:
+                nc.scalar.activation(a_n7[:, t, half_cols(h)], a[t][:].indirect(half_list(l_n7, h)), ACT.Copy)
+        z2_second_product(1)
+        b_product(0)
         z2_round(1)
-        z2_matmul(1)
-        copy_b(1)
-        gather_a(2)
-        gather_a(3)
+        b_product(1)
 
-        QUART = S // 4
-        m7 = [keep.tile([P, PACK, HALF], F32, name=f"m7_{h}") for h in range(2)]
-        m8 = [keep.tile([P, PACK, HALF], F32, name=f"m8_{h}") for h in range(2)]
-        b8 = [keep.tile([P, PACK, HALF], F32, name=f"bn8_{h}") for h in range(2)]
-        osc = keep.tile([P, S], U8, name="osc", align_bytes=64)
+        term_7 = [keep.tile([P, PACK, HALF], F32, name=f"term_7_{h}") for h in halves]
+        for h in halves:
+            for u in range(2):
+                pair = slice(2 * u, 2 * u + 2)
+                nc.vector.tensor_tensor(term_7[h][:, pair, :], a_n7[:, pair, half_cols(h)], b_bank[h, u][:], MULT)
+                for e in range(2):
+                    nc.scalar.copy(b[2 * u + e][:, half_cols(h)], b_bank[h, u][:, e, :])
+
+        term_8 = [keep.tile([P, PACK, HALF], F32, name=f"term_8_{h}") for h in halves]
+        b_n8 = [keep.tile([P, PACK, HALF], F32, name=f"b_n8_{h}") for h in halves]
+        o_s = keep.tile([P, S], U8, name="o_s", align_bytes=64)
         out_rows = out_0.rearrange("(p t) s -> p t s", t=PACK)
-        out_words = out_1[0].rearrange("p n t -> p (n t)").bitcast(I32)
-
-        def times_b(h, u):
-            ts = slice(2 * u, 2 * u + 2)
-            nc.vector.tensor_tensor(m7[h][:, ts, :], a7[:, ts, half_cols(h)], bbank[h, u][:], MULT)
-
-        times_b(0, 0)
-        times_b(1, 0)
-        FUSED = 1
+        out_words = as_words(out_1)
 
         def gather_b(h, t):
-            nc.scalar.activation(b8[h][:, t, :], b[t][:].indirect(half_list(l_n8, h)), ACT.Copy)
+            nc.scalar.activation(b_n8[h][:, t, :], b[t][:].indirect(half_list(l_n8, h)), ACT.Copy)
 
         def times_a(h, t):
-            nc.vector.tensor_tensor(m8[h][:, t, :], b8[h][:, t, :], a[t][:, half_cols(h)], MULT)
+            nc.vector.tensor_tensor(term_8[h][:, t, :], b_n8[h][:, t, :], a[t][:, half_cols(h)], MULT)
 
-        for t in range(FUSED, PACK):
+        for t in range(FUSED_N8, PACK):
             gather_b(0, t)
-        for t in range(PACK):
+        for t in planes:
             gather_b(1, t)
-        for t in range(FUSED):
-            nc.vector.tensor_tensor(m8[0][:, t, :], b[t][:].indirect(half_list(l_n8, 0)), a[t][:, half_cols(0)], MULT)
-        times_b(0, 1)
-        times_b(1, 1)
-        for t in range(FUSED, PACK):
+        for t in range(FUSED_N8):
+            gather_times(term_8[0][:, t, :], b[t], l_n8, a[t][:, half_cols(0)], 0)
+        for t in range(FUSED_N8, PACK):
             times_a(0, t)
 
-        def finish(name, h, lo, width, weave):
-            cols = slice(h * HALF + lo, h * HALF + lo + width)
-            of = keep.tile([P, PACK, width], F32, name="of" + name)
-            ob = keep.tile([P, width * PACK], BF16, name="ob" + name, align_bytes=64)
-            nc.vector.tensor_tensor(of[:], m8[h][:, :, lo : lo + width], m7[h][:, :, lo : lo + width], SUB)
-            nc.sync.dma_start(out_rows[:, :, cols], of[:])
-            weave(woven(ob[:]), planar(of[:]))
-            return name, cols, width, ob
+        def subtract_and_round(first_col, width, weave):
+            h, lo = divmod(first_col, HALF)
+            o_f32 = keep.tile([P, PACK, width], F32, name=f"o_f32_{first_col}")
+            o_bf = keep.tile([P, width * PACK], BF16, name=f"o_bf_{first_col}", align_bytes=64)
+            nc.vector.tensor_tensor(o_f32[:], term_8[h][:, :, lo : lo + width], term_7[h][:, :, lo : lo + width], SUB)
+            nc.sync.dma_start(out_rows[:, :, first_col : first_col + width], o_f32[:])
+            weave(woven(o_bf[:]), planar(o_f32[:]))
+            return first_col, width, o_bf
 
-        def planes(name, cols, width, ob):
-            ow = keep.tile([P, width], U32, name="ow" + name, align_bytes=64)
-            nc.vector.quantize_mx(out=ow[:].bitcast(FP8X4), scales=osc[:, cols], in_=ob[:])
-            nc.sync.dma_start(out_words[:, cols], ow[:].bitcast(I32))
+        def quantise_and_store(first_col, width, o_bf):
+            cols = slice(first_col, first_col + width)
+            o_w = keep.tile([P, width], U32, name=f"o_w_{first_col}", align_bytes=64)
+            nc.vector.quantize_mx(out=o_w[:].bitcast(FP8X4), scales=o_s[:, cols], in_=o_bf[:])
+            nc.sync.dma_start(out_words[:, cols], o_w[:].bitcast(I32))
 
-        first = finish("a", 0, 0, HALF, nc.scalar.copy)
-        for t in range(PACK):
+        first_half = subtract_and_round(0, HALF, nc.scalar.copy)
+        for t in planes:
             times_a(1, t)
-        second = finish("b", 1, 0, QUART, nc.scalar.copy)
-        planes(*first)
-        third = finish("c", 1, QUART, QUART, nc.vector.tensor_copy)
-        planes(*second)
-        planes(*third)
-        for q in range(4):
-            nc.sync.dma_start(out_2[0, 4 * q : 4 * q + 4, :].bitcast(I32), osc[32 * q : 32 * q + 4, :].bitcast(I32))
+        third_quarter = subtract_and_round(HALF, QUART, nc.scalar.copy)
+        quantise_and_store(*first_half)
+        last_quarter = subtract_and_round(HALF + QUART, QUART, nc.vector.tensor_copy)
+        quantise_and_store(*third_quarter)
+        quantise_and_store(*last_quarter)
+        for q in range(QUADS):
+            nc.sync.dma_start(out_2[0, 4 * q : 4 * q + 4, :].bitcast(I32), o_s[32 * q : 32 * q + 4, :].bitcast(I32))

from contextlib import ExitStack

import concourse.mybir as mybir

K, T, S, H, C = 512, 2048, 512, 512, 512
FLOPS = 2 * K * S * (H + 2 * C)

F32 = mybir.dt.float32
BF16 = mybir.dt.bfloat16
I32 = mybir.dt.int32
U32 = mybir.dt.uint32
U16 = mybir.dt.uint16
U8 = mybir.dt.uint8
FP8X4 = mybir.dt.float8_e4m3fn_x4
ACT = mybir.ActivationFunctionType
MULT = mybir.AluOpType.mult
ADD = mybir.AluOpType.add
SUB = mybir.AluOpType.subtract

P = 128
PACK = 4
QUADS = 4
HALF = S // 2
QUART = S // 4
LIST_COLS = S // 16
SPARE = 16
WORD_RUN = 4
BYTE_RUN = 16
OUT_SCALE = 0.75 * 0.0625 * 0.0625
FUSED_N8 = 3


def tile_picked_twocdcrossbrmsdet_none_po_kernel(
    tc, x_words, x_scales, w1_words, w1_scales, gs, gs2, offs, n1, n2, n3, n4, n5, n6, ca, cb, n7, n8,
    out_0, out_1, out_2,
):
    nc = tc.nc
    planes = range(PACK)
    halves = range(2)
    with ExitStack() as ctx:
        keep = ctx.enter_context(tc.tile_pool(name="keep", bufs=1))
        psum = ctx.enter_context(tc.psum_pool(name="psum", bufs=1))

        def load_list(name, src):
            tile = keep.tile([P, LIST_COLS], U16, name="list_" + name)
            nc.sync.dma_start(tile[:], src)
            return tile

        def load_scales(queues, tile, src):
            for q, queue in enumerate(queues):
                rows = src[0, 4 * q : 4 * q + 4, :].bitcast(I32)
                queue.dma_start(tile[32 * q : 32 * q + 32, :].bitcast(I32), rows.partition_broadcast(8))

        def as_words(dram):
            return dram[0].rearrange("p n t -> p (n t)").bitcast(I32)

        def half_cols(h):
            return slice(h * HALF, (h + 1) * HALF)

        def half_list(lst, h):
            return lst[:, h * (LIST_COLS // 2) : (h + 1) * (LIST_COLS // 2)]

        def deal(dst, src, run):
            nc.vector.tensor_copy(
                out=dst.rearrange("p (g t c i) -> p g c t i", t=PACK, c=P // run, i=run),
                in_=src.rearrange("p (g c i t) -> p g c t i", t=PACK, c=P // run, i=run),
            )

        def woven(ap):
            return ap.rearrange("p (c i t) -> p c t i", i=WORD_RUN, t=PACK)

        def planar(ap):
            return ap.rearrange("p t (c i) -> p c t i", i=WORD_RUN)

        def mx_pass(out, lhs_words, lhs_scales, cols, rhs_words, rhs_scales):
            nc.tensor.matmul_mx(
                out=out, lhsT=lhs_words[:, cols].bitcast(FP8X4), lhsT_scale=lhs_scales[:, cols],
                rhs=rhs_words[:].bitcast(FP8X4), rhs_scale=rhs_scales[:], start=True, stop=True,
            )

        x_s = keep.tile([P, T], U8, name="x_s", align_bytes=64)
        x_w = keep.tile([P, T], U32, name="x_w", align_bytes=64)
        w_w = keep.tile([P, H], U32, name="w_w", align_bytes=64)
        w_s = keep.tile([P, H], U8, name="w_s", tag="staged", align_bytes=64)
        load_scales([nc.sync] * QUADS, x_s, x_scales)
        l_offs = load_list("offs", offs)
        l_ca = load_list("ca", ca)
        nc.sync.dma_start(w_w[:].bitcast(I32), as_words(w1_words))
        nc.sync.dma_start(x_w[:].bitcast(I32), as_words(x_words))
        load_scales([nc.sync] + [nc.gpsimd] * (QUADS - 1), w_s, w1_scales)
        l_cb = load_list("cb", cb)
        gain_z = keep.tile([P, PACK], F32, name="gain_z")
        gain_z2_in = keep.tile([P, PACK], F32, name="gain_z2_in")
        nc.sync.dma_start(gain_z[:], gs.rearrange("(p t) o -> p (t o)", t=PACK))
        nc.sync.dma_start(gain_z2_in[:], gs2.rearrange("(p t) o -> p (t o)", t=PACK))
        l_n1 = load_list("n1", n1)
        l_n3 = load_list("n3", n3)
        l_n5 = load_list("n5", n5)
        l_n2 = load_list("n2", n2)
        l_n4 = load_list("n4", n4)
        l_n6 = load_list("n6", n6)
        l_n7 = load_list("n7", n7)
        l_n8 = load_list("n8", n8)

        sq = [keep.tile([P, S + SPARE], F32, name=f"sq{t}", align_bytes=64) for t in planes]
        y_gs = [keep.tile([P, S + SPARE], F32, name=f"y_gs{t}") for t in planes]
        for t in planes:
            nc.gpsimd.memset(sq[t][:, S:], 0.0)
            nc.gpsimd.memset(y_gs[t][:, S:], 0.0)

        warm = keep.tile([P, 2], F32, name="warm")
        nc.vector.memset(warm[:, 0:1], 1.0)
        nc.scalar.activation(warm[:, 1:2], warm[:, 0:1], ACT.Abs_reciprocal_sqrt)

        q_w = keep.tile([P, S], U32, name="q_w", align_bytes=64)
        q_s = keep.tile([P, S], U8, name="q_s", align_bytes=64)
        c_s = keep.tile([P, 2 * C], U8, name="c_s", align_bytes=64)
        w_w_dealt = keep.tile([P, H], U32, name="w_w_dealt", align_bytes=64)
        w_s_dealt = keep.tile([P, H], U8, name="w_s_dealt", align_bytes=64)
        nc.vector.tensor_copy(q_s[:], x_s[:].indirect(l_offs[:]))
        deal(w_w_dealt[:], w_w[:], WORD_RUN)
        nc.vector.tensor_copy(q_w[:], x_w[:].indirect(l_offs[:]))
        nc.vector.tensor_copy(c_s[:, :C], x_s[:].indirect(l_ca[:]))
        deal(w_s_dealt[:], w_s[:], BYTE_RUN)
        gain_z2 = keep.tile([P, PACK], F32, name="gain_z2")
        nc.gpsimd.tensor_scalar(gain_z2[:], gain_z2_in[:], 0.75, 0.0, MULT, ADD)

        y = [keep.tile([P, S], F32, name=f"y{t}") for t in planes]
        y_gs2 = [keep.tile([P, 2 * S], F32, name=f"y_gs2_{t}") for t in planes]
        a = [keep.tile([P, S], F32, name=f"a{t}") for t in planes]
        y_bank = []
        for t in planes:
            bank = psum.tile([P, S], F32, name=f"y_bank{t}", tag=f"yb_bank{t}")
            y_bank.append(bank)
            mx_pass(bank[:], w_w_dealt, w_s_dealt, slice(t * P, (t + 1) * P), q_w, q_s)
            nc.scalar.activation(sq[t][:, :S], bank[:], ACT.Square)
            nc.sync.dma_start(y_gs2[t][:, S:], sq[t][:, :S])
        for t in planes:
            nc.scalar.copy(y[t][:], y_bank[t][:])

        c_w = keep.tile([P, 2 * C], U32, name="c_w", tag="staged", align_bytes=64)
        nc.vector.tensor_copy(c_w[:, :C], x_w[:].indirect(l_ca[:]))
        nc.vector.tensor_copy(c_w[:, C:], x_w[:].indirect(l_cb[:]))

        inv_root = keep.tile([P, PACK, S], F32, name="inv_root")
        y_n2 = keep.tile([P, PACK, S], F32, name="y_n2", tag="rows0")
        sq_sum = keep.tile([P, PACK, S], F32, name="sq_sum", tag="rows1")
        prod_34 = keep.tile([P, PACK, S], F32, name="prod_34")
        for t in planes:
            nc.vector.tensor_scalar(y_gs[t][:, :S], y[t][:], gain_z[:, t : t + 1], None, MULT)
        for t in planes:
            nc.vector.tensor_scalar(y_gs2[t][:, :S], y[t][:], gain_z2[:, t : t + 1], None, MULT)
        nc.vector.tensor_copy(c_s[:, C:], x_s[:].indirect(l_cb[:]))
        for t in planes:
            nc.vector.tensor_tensor(sq_sum[:, t, :], sq[t][:].indirect(l_n1[:]), y_gs2[t][:, S:], ADD)
        for t in planes:
            nc.scalar.activation(y_n2[:, t, :], y_gs[t][:].indirect(l_n2[:]), ACT.Copy)
        for t in planes:
            nc.scalar.activation(inv_root[:, t, :], sq_sum[:, t, :], ACT.Abs_reciprocal_sqrt, bias=0.25)

        c_w_dealt = keep.tile([P, 2 * C], U32, name="c_w_dealt", tag=f"sq{PACK - 1}", align_bytes=64)
        c_s_dealt = keep.tile([P, 2 * C], U8, name="c_s_dealt", tag=f"sq{PACK - 2}", align_bytes=64)
        deal(c_w_dealt[:], c_w[:], WORD_RUN)
        deal(c_s_dealt[:], c_s[:], BYTE_RUN)
        z_bf = keep.tile([P, S * PACK], BF16, name="z_bf", align_bytes=64)
        z_w = keep.tile([P, S], U32, name="z_w", align_bytes=64)
        z_s = keep.tile([P, S], U8, name="z_s", align_bytes=64)
        nc.vector.tensor_tensor(woven(z_bf[:]), planar(y_n2[:]), planar(inv_root[:]), MULT)

        y_n3 = keep.tile([P, PACK, S], F32, name="y_n3", tag="rows1")
        y_n5 = keep.tile([P, PACK, S], F32, name="y_n5", tag="rows0")
        for t in planes:
            nc.scalar.activation(y_n3[:, t, :], y_gs2[t][:].indirect(l_n3[:]), ACT.Copy)
        for t in planes:
            nc.scalar.activation(y_n5[:, t, :], y_gs2[t][:].indirect(l_n5[:]), ACT.Copy)
        nc.vector.quantize_mx(out=z_w[:].bitcast(FP8X4), scales=z_s[:], in_=z_bf[:])

        b = [keep.tile([P, S], F32, name=f"b{t}") for t in planes]
        a_n7 = keep.tile([P, PACK, S], F32, name="a_n7")
        for t in planes:
            bank = psum.tile([P, S], F32, name=f"a_bank{t}")
            mx_pass(bank[:], c_w_dealt, c_s_dealt, slice(t * P, (t + 1) * P), z_w, z_s)
            nc.scalar.activation(a[t][:], bank[:], ACT.Copy, scale=OUT_SCALE)

        prod_56 = keep.tile([P, PACK, S], F32, name="prod_56")
        z2_bf = [keep.tile([P, HALF * PACK], BF16, name=f"z2_bf{h}", align_bytes=64) for h in halves]
        z2_w = [keep.tile([P, HALF], U32, name=f"z2_w{h}", align_bytes=64) for h in halves]
        z2_s = [keep.tile([P, HALF], U8, name=f"z2_s{h}", align_bytes=64) for h in halves]
        b_bank = {}

        def gather_times(dst, window, lst, other, h):
            nc.vector.tensor_tensor(dst, window[:].indirect(half_list(lst, h)), other, MULT)

        def z2_second_product(h):
            for t in planes:
                gather_times(prod_56[:, t, half_cols(h)], y[t], l_n6, y_n5[:, t, half_cols(h)], h)

        def z2_round(h):
            cols = half_cols(h)
            nc.vector.tensor_tensor(woven(z2_bf[h][:]), planar(prod_34[:, :, cols]), planar(prod_56[:, :, cols]), SUB)

        def b_product(h):
            nc.vector.quantize_mx(out=z2_w[h][:].bitcast(FP8X4), scales=z2_s[h][:], in_=z2_bf[h][:])
            for u in range(2):
                bank = psum.tile([P, 2, HALF], F32, name=f"b_bank{h}{u}", tag=f"yb_bank{2 * h + u}")
                b_bank[h, u] = bank
                for e in range(2):
                    first_col = C + (2 * u + e) * P
                    mx_pass(bank[:, e, :], c_w_dealt, c_s_dealt, slice(first_col, first_col + P), z2_w[h], z2_s[h])

        for t in planes:
            for h in halves:
                gather_times(prod_34[:, t, half_cols(h)], y[t], l_n4, y_n3[:, t, half_cols(h)], h)
        z2_second_product(0)
        z2_round(0)
        for t in planes:
            for h in halves:
                nc.scalar.activation(a_n7[:, t, half_cols(h)], a[t][:].indirect(half_list(l_n7, h)), ACT.Copy)
        z2_second_product(1)
        b_product(0)
        z2_round(1)
        b_product(1)

        term_7 = [keep.tile([P, PACK, HALF], F32, name=f"term_7_{h}") for h in halves]
        for h in halves:
            for u in range(2):
                pair = slice(2 * u, 2 * u + 2)
                nc.vector.tensor_tensor(term_7[h][:, pair, :], a_n7[:, pair, half_cols(h)], b_bank[h, u][:], MULT)
                for e in range(2):
                    nc.scalar.copy(b[2 * u + e][:, half_cols(h)], b_bank[h, u][:, e, :])

        term_8 = [keep.tile([P, PACK, HALF], F32, name=f"term_8_{h}") for h in halves]
        b_n8 = [keep.tile([P, PACK, HALF], F32, name=f"b_n8_{h}") for h in halves]
        o_s = keep.tile([P, S], U8, name="o_s", align_bytes=64)
        out_rows = out_0.rearrange("(p t) s -> p t s", t=PACK)
        out_words = as_words(out_1)

        def gather_b(h, t):
            nc.scalar.activation(b_n8[h][:, t, :], b[t][:].indirect(half_list(l_n8, h)), ACT.Copy)

        def times_a(h, t):
            nc.vector.tensor_tensor(term_8[h][:, t, :], b_n8[h][:, t, :], a[t][:, half_cols(h)], MULT)

        for t in range(FUSED_N8, PACK):
            gather_b(0, t)
        for t in planes:
            gather_b(1, t)
        for t in range(FUSED_N8):
            gather_times(term_8[0][:, t, :], b[t], l_n8, a[t][:, half_cols(0)], 0)
        for t in range(FUSED_N8, PACK):
            times_a(0, t)

        def subtract_and_round(first_col, width, weave):
            h, lo = divmod(first_col, HALF)
            o_f32 = keep.tile([P, PACK, width], F32, name=f"o_f32_{first_col}")
            o_bf = keep.tile([P, width * PACK], BF16, name=f"o_bf_{first_col}", align_bytes=64)
            nc.vector.tensor_tensor(o_f32[:], term_8[h][:, :, lo : lo + width], term_7[h][:, :, lo : lo + width], SUB)
            nc.sync.dma_start(out_rows[:, :, first_col : first_col + width], o_f32[:])
            weave(woven(o_bf[:]), planar(o_f32[:]))
            return first_col, width, o_bf

        def quantise_and_store(first_col, width, o_bf):
            cols = slice(first_col, first_col + width)
            o_w = keep.tile([P, width], U32, name=f"o_w_{first_col}", align_bytes=64)
            nc.vector.quantize_mx(out=o_w[:].bitcast(FP8X4), scales=o_s[:, cols], in_=o_bf[:])
            nc.sync.dma_start(out_words[:, cols], o_w[:].bitcast(I32))

        first_half = subtract_and_round(0, HALF, nc.scalar.copy)
        for t in planes:
            times_a(1, t)
        third_quarter = subtract_and_round(HALF, QUART, nc.scalar.copy)
        quantise_and_store(*first_half)
        last_quarter = subtract_and_round(HALF + QUART, QUART, nc.vector.tensor_copy)
        quantise_and_store(*third_quarter)
        quantise_and_store(*last_quarter)
        for q in range(QUADS):
            nc.sync.dma_start(out_2[0, 4 * q : 4 * q + 4, :].bitcast(I32), o_s[32 * q : 32 * q + 4, :].bitcast(I32))
